import numpy as np
CORES = [50,51,178,179,306,307,434,435]
N = 8
GROUPS = [[0,1,2,3],[4,5,6,7]]
def setup_inputs(rng):
    return {"x": rng.standard_normal((N, 128, 64), dtype=np.float32)}
def reference(x):
    y = np.empty((N, 128, 256), x.dtype)
    for g in GROUPS:
        s = np.concatenate([x[r] for r in g], axis=1)
        for r in g:
            y[r] = s
    return {"y": y}

@@ -1,0 +1,71 @@
+from concourse.bass import DstId, RemoteDMATransfer
+
+W = 64
+
+SCRATCH = {
+    "stage": ("dram", [128, W], "float32"),
+    "land": ("dram", [3, 128, W], "float32"),
+}
+SEMAPHORES = ["loaded", "sent", "arr0", "arr1", "arr2", "st_own", "st0", "st1", "st2"]
+
+
+def _slot(group, receiver, sender):
+    return [m for m in group if m != receiver].index(sender)
+
+
+def _same_chip(topo, a, b):
+    return topo.host(a) == topo.host(b) and topo.chip(a) == topo.chip(b)
+
+
+def _engines(topo, cores, group, sender):
+    far_masks = [0x000F, 0x00F0]
+    out = {}
+    for m in group:
+        if m == sender:
+            continue
+        if _same_chip(topo, cores[sender], cores[m]):
+            out[m] = 0xFF00
+        else:
+            out[m] = far_masks.pop(0)
+    return out
+
+
+def rank_program(g, core, T, topo):
+    rank = T.rank_of(core)
+    if rank is None:
+        return
+    cores = T.cores
+    group = [grp for grp in T.tables["GROUPS"] if rank in grp][0]
+    pos = group.index(rank)
+
+    g.sync.dma_start(T.stage[:], T.x[:]).then_inc(T.sem.loaded, 16)
+    g.sync.dma_start(T.y[:, pos * W:(pos + 1) * W], T.x[:]).then_inc(T.sem.st_own, 16)
+
+    g.wait_ge(T.sem.loaded, 16)
+    transfers = []
+    sent = 0
+    for m, mask in _engines(topo, cores, group, rank).items():
+        rid, pid = topo.addr(cores[m], core)
+        k = _slot(group, m, rank)
+        transfers.append(RemoteDMATransfer(
+            dst_ids=[DstId(rid=rid, pnc=pid)], dma_engine_mask=mask, remote_sem=T.sem["arr%d" % k],
+            src=T.stage[:], dst=T.land[k]))
+        sent += bin(mask).count("1")
+    g.remote_dma_fused(transfers, local_sem=T.sem.sent)
+
+    near = [m for m in group if m != rank and _same_chip(topo, cores[m], core)]
+    far = [m for m in group if m != rank and not _same_chip(topo, cores[m], core)]
+    plan = [(m, g.scalar) for m in near]
+    for i, m in enumerate(far):
+        plan.append((m, g.sync if i % 2 == 0 else g.scalar))
+    for m, q in plan:
+        k = _slot(group, rank, m)
+        n = bin(_engines(topo, cores, group, m)[rank]).count("1")
+        p = group.index(m)
+        q.wait_ge(T.sem["arr%d" % k], n)
+        q.dma_start(T.y[:, p * W:(p + 1) * W], T.land[k]).then_inc(T.sem["st%d" % k], 16)
+
+    g.wait_ge(T.sem.sent, sent)
+    g.wait_ge(T.sem.st_own, 16)
+    for k in range(len(group) - 1):
+        g.wait_ge(T.sem["st%d" % k], 16)

@@ -17,17 +17,9 @@ def _same_chip(topo, a, b):
     return topo.host(a) == topo.host(b) and topo.chip(a) == topo.chip(b)
 
 
-def _engines(topo, cores, group, sender):
-    far_masks = [0x000F, 0x00F0]
-    out = {}
-    for m in group:
-        if m == sender:
-            continue
-        if _same_chip(topo, cores[sender], cores[m]):
-            out[m] = 0xFF00
-        else:
-            out[m] = far_masks.pop(0)
-    return out
+def _far(topo, cores, group, rank):
+    far = [m for m in group if not _same_chip(topo, cores[m], cores[rank])]
+    return sorted(far, key=lambda m: (cores[m] % 8 != cores[rank] % 8, m))
 
 
 def rank_program(g, core, T, topo):
@@ -37,35 +29,31 @@ def rank_program(g, core, T, topo):
     cores = T.cores
     group = [grp for grp in T.tables["GROUPS"] if rank in grp][0]
     pos = group.index(rank)
+    near = [m for m in group if m != rank and _same_chip(topo, cores[m], core)]
+    far = _far(topo, cores, group, rank)
 
     g.sync.dma_start(T.stage[:], T.x[:]).then_inc(T.sem.loaded, 16)
     g.sync.dma_start(T.y[:, pos * W:(pos + 1) * W], T.x[:]).then_inc(T.sem.st_own, 16)
 
     g.wait_ge(T.sem.loaded, 16)
     transfers = []
-    sent = 0
-    for m, mask in _engines(topo, cores, group, rank).items():
-        rid, pid = topo.addr(cores[m], core)
-        k = _slot(group, m, rank)
+    for members, mask in ((far, 0x00FF), (near, 0xFF00)):
+        ks = [_slot(group, m, rank) for m in members]
+        assert len(set(ks)) == 1
+        ids = [topo.addr(cores[m], core) for m in members]
         transfers.append(RemoteDMATransfer(
-            dst_ids=[DstId(rid=rid, pnc=pid)], dma_engine_mask=mask, remote_sem=T.sem["arr%d" % k],
-            src=T.stage[:], dst=T.land[k]))
-        sent += bin(mask).count("1")
+            dst_ids=[DstId(rid=rid, pnc=pid) for rid, pid in ids], dma_engine_mask=mask,
+            remote_sem=T.sem["arr%d" % ks[0]], srcs=[T.stage[:]], dsts=[T.land[k] for k in ks]))
     g.remote_dma_fused(transfers, local_sem=T.sem.sent)
 
-    near = [m for m in group if m != rank and _same_chip(topo, cores[m], core)]
-    far = [m for m in group if m != rank and not _same_chip(topo, cores[m], core)]
-    plan = [(m, g.scalar) for m in near]
-    for i, m in enumerate(far):
-        plan.append((m, g.sync if i % 2 == 0 else g.scalar))
+    plan = [(m, g.scalar) for m in near] + [(far[0], g.sync), (far[1], g.scalar)]
     for m, q in plan:
         k = _slot(group, rank, m)
-        n = bin(_engines(topo, cores, group, m)[rank]).count("1")
         p = group.index(m)
-        q.wait_ge(T.sem["arr%d" % k], n)
+        q.wait_ge(T.sem["arr%d" % k], 8)
         q.dma_start(T.y[:, p * W:(p + 1) * W], T.land[k]).then_inc(T.sem["st%d" % k], 16)
 
-    g.wait_ge(T.sem.sent, sent)
+    g.wait_ge(T.sem.sent, 16)
     g.wait_ge(T.sem.st_own, 16)
     for k in range(len(group) - 1):
         g.wait_ge(T.sem["st%d" % k], 16)

from concourse.bass import DstId, RemoteDMATransfer

W = 64

SCRATCH = {
    "stage": ("dram", [128, W], "float32"),
    "land": ("dram", [3, 128, W], "float32"),
}
SEMAPHORES = ["loaded", "sent", "arr0", "arr1", "arr2", "st_own", "st0", "st1", "st2"]


def _slot(group, receiver, sender):
    return [m for m in group if m != receiver].index(sender)


def _same_chip(topo, a, b):
    return topo.host(a) == topo.host(b) and topo.chip(a) == topo.chip(b)


def _far(topo, cores, group, rank):
    far = [m for m in group if not _same_chip(topo, cores[m], cores[rank])]
    return sorted(far, key=lambda m: (cores[m] % 8 != cores[rank] % 8, m))


def rank_program(g, core, T, topo):
    rank = T.rank_of(core)
    if rank is None:
        return
    cores = T.cores
    group = [grp for grp in T.tables["GROUPS"] if rank in grp][0]
    pos = group.index(rank)
    near = [m for m in group if m != rank and _same_chip(topo, cores[m], core)]
    far = _far(topo, cores, group, rank)

    g.sync.dma_start(T.stage[:], T.x[:]).then_inc(T.sem.loaded, 16)
    g.sync.dma_start(T.y[:, pos * W:(pos + 1) * W], T.x[:]).then_inc(T.sem.st_own, 16)

    g.wait_ge(T.sem.loaded, 16)
    transfers = []
    for members, mask in ((far, 0x00FF), (near, 0xFF00)):
        ks = [_slot(group, m, rank) for m in members]
        assert len(set(ks)) == 1
        ids = [topo.addr(cores[m], core) for m in members]
        transfers.append(RemoteDMATransfer(
            dst_ids=[DstId(rid=rid, pnc=pid) for rid, pid in ids], dma_engine_mask=mask,
            remote_sem=T.sem["arr%d" % ks[0]], srcs=[T.stage[:]], dsts=[T.land[k] for k in ks]))
    g.remote_dma_fused(transfers, local_sem=T.sem.sent)

    plan = [(m, g.scalar) for m in near] + [(far[0], g.sync), (far[1], g.scalar)]
    for m, q in plan:
        k = _slot(group, rank, m)
        p = group.index(m)
        q.wait_ge(T.sem["arr%d" % k], 8)
        q.dma_start(T.y[:, p * W:(p + 1) * W], T.land[k]).then_inc(T.sem["st%d" % k], 16)

    g.wait_ge(T.sem.sent, 16)
    g.wait_ge(T.sem.st_own, 16)
    for k in range(len(group) - 1):
        g.wait_ge(T.sem["st%d" % k], 16)
